import numpy as np
import ml_dtypes


def mxq(x, axis, fmt="e4m3"):
    dtype, down = {"e4m3": (ml_dtypes.float8_e4m3fn, 7), "e5m2": (ml_dtypes.float8_e5m2, 14)}[fmt]
    v = np.moveaxis(np.asarray(x, np.float32).astype(ml_dtypes.bfloat16).astype(np.float64), axis, -1)
    blocks = v.reshape(v.shape[:-1] + (-1, 32))
    amax = np.abs(blocks).max(-1, keepdims=True)
    byte = np.maximum(np.where(amax > 0, np.frexp(amax)[1] - 1 + 127, 0) - down, 1)
    scale = np.exp2(byte - 127.0)
    codes = (blocks / scale).astype(np.float32).astype(dtype).astype(np.float64)
    return np.moveaxis((codes * scale).reshape(v.shape), -1, axis)


WIDE = False


def mx_kscale(k):
    if not WIDE:
        return np.ones(k)
    levels = np.array([10, -10, 5, -5, 0])
    if k % 512:
        return np.exp2(np.random.permutation(np.resize(levels, k // 32))).repeat(32)
    a = np.empty((k // 512, 16))
    for p in range(k // 512):
        a[p, :8] = np.random.permutation(np.resize(levels, 8))
        for g in range(8):
            far = levels[np.abs(levels - a[p, g]) >= 10]
            a[p, g + 8] = far[np.random.randint(len(far))]
    return np.exp2(a.ravel()).repeat(32)


def f64(x):
    return np.asarray(x).astype(np.float64)


def striped(idx):
    return np.tile(idx.reshape(-1, 16).T, (8, 1)).astype(np.uint16)


def unstriped(offs):
    return offs[:16].T.reshape(-1).astype(np.int64)


E2M1 = np.array([0.0, 0.5, 1.0, 1.5, 2.0, 3.0, 4.0, 6.0, -0.0, -0.5, -1.0, -1.5, -2.0, -3.0, -4.0, -6.0])


def pack_weight(w, fmt):
    k, n = w.shape
    w = f64(np.asarray(w, np.float32).astype(ml_dtypes.bfloat16)).reshape(k // 32, 32, n)
    amax = np.abs(w).max(1)
    if fmt == "e4m3":
        byte = np.frexp(amax)[1] - 1 + 127 - 7
    else:
        mant, ex = np.frexp(amax / 6.0)
        byte = np.where(mant > 0.5, ex, ex - 1) + 127
    byte = np.clip(np.where(amax > 0, byte, 1), 1, 254)
    scaled = (w * np.exp2(127.0 - byte)[:, None, :]).reshape(k, n).astype(np.float32)
    by_word = np.ascontiguousarray(scaled.reshape(k // 512, 128, 4, n).transpose(0, 1, 3, 2))
    if fmt == "e4m3":
        words = by_word.astype(ml_dtypes.float8_e4m3fn).view(np.uint8)
    else:
        c = by_word.astype(ml_dtypes.float4_e2m1fn).view(np.uint8) & 0xF
        words = (c[..., 0::2] | (c[..., 1::2] << 4)).reshape(k // 512, 128, 2 * n)
    return np.ascontiguousarray(words), np.ascontiguousarray(byte.astype(np.uint8).reshape(k // 512, 16, n))


def unpack_weight(words, scales, fmt):
    g, _, n = scales.shape
    words = np.ascontiguousarray(words).reshape(g, 128, n, -1)
    if fmt == "e4m3":
        vals = words.view(ml_dtypes.float8_e4m3fn).astype(np.float64)
    else:
        nib = np.empty((g, 128, n, 4), np.uint8)
        nib[..., 0::2] = words & 0xF
        nib[..., 1::2] = words >> 4
        vals = E2M1[nib]
    vals = vals * np.repeat(np.exp2(scales.astype(np.float64) - 127.0), 8, axis=1)[..., None]
    return vals.transpose(0, 1, 3, 2).reshape(g * 512, n)


def gelu(v):
    return 0.5 * v * (1.0 + np.tanh(np.sqrt(2.0 / np.pi) * (v + 0.044715 * v**3)))


def bf(x):
    return np.asarray(x, np.float32).astype(ml_dtypes.bfloat16)


def planes(Y):
    n, m = Y.shape
    b = f64(bf(Y)).reshape(n // 32, 32, m)
    amax = np.abs(b).max(1)
    byte = np.clip(np.where(amax > 0, np.frexp(amax)[1] - 1 + 127 - 7, 1), 1, 254)
    codes = (b * np.exp2(127.0 - byte)[:, None, :]).reshape(n, m).astype(np.float32).astype(ml_dtypes.float8_e4m3fn).view(np.uint8)
    words = codes.reshape(n // 512, 128, 4, m).transpose(0, 1, 3, 2)
    return np.ascontiguousarray(words), np.ascontiguousarray(byte.astype(np.uint8).reshape(n // 512, 16, m))


K, T, S, H, N, T2, P = 1536, 2048, 1024, 512, 768, 2048, 1024

def setup_inputs():
    n = np.random.standard_normal
    s = mx_kscale(K)[:, None]
    u = mx_kscale(H)[:, None]
    d = {}
    d["tab_words"], d["tab_scales"] = pack_weight(n((K, T)) * s, "e4m3")
    d["offs"] = striped(np.random.permutation(T)[:S])
    d["offs2"] = striped(np.random.permutation(T2)[:S])
    d["offs3"] = striped(np.random.permutation(T2)[:P])
    d["w1"] = (n((K, H)) / K ** 0.5 / s * u.T).astype(np.float32)
    d["base"] = (0.7 * n(H) * u[:, 0]).astype(np.float32)
    d["wgs"] = np.exp(0.3 * n((128, S))).astype(np.float32)
    d["page0"] = (n((H, T2)) * u).astype(np.float32)
    d["w2"] = (n((H, N)) / H ** 0.5 / u).astype(np.float32)
    d["w3_words"], d["w3_scales"] = pack_weight(n((K, N)) / K ** 0.5 / s, "e2m1")
    return d

def reference(tab_words, tab_scales, offs, offs2, offs3, w1, base, wgs, page0, w2, w3_words, w3_scales):
    v = unpack_weight(tab_words, tab_scales, "e4m3")[:, unstriped(offs)]
    h = (mxq(f64(w1), 0, "e4m3").T @ v) - f64(base)[:, None]
    page = f64(page0).copy()
    page[:, unstriped(offs2)] = np.tile(f64(wgs), (H // 128, 1)) * h
    x = np.abs(page[:, unstriped(offs3)])
    cells = mxq(f64(w2), 0, "e4m3").T @ mxq(x, 0, "e4m3")
    caps = unpack_weight(w3_words, w3_scales, "e2m1").T @ v
    y = cells * caps
    words, scales = planes(page)
    return y, page, words, scales

@@ -1,0 +1,321 @@
+from contextlib import ExitStack
+
+import concourse.mybir as mybir
+
+K, T, S, H, N, T2 = 1536, 2048, 1024, 512, 768, 2048
+FLOPS = 2 * S * (K * H + H * N + K * N)
+
+F32 = mybir.dt.float32
+BF16 = mybir.dt.bfloat16
+I32 = mybir.dt.int32
+U32 = mybir.dt.uint32
+U16 = mybir.dt.uint16
+U8 = mybir.dt.uint8
+FP8X4 = mybir.dt.float8_e4m3fn_x4
+FP4X4 = mybir.dt.float4_e2m1fn_x4
+ACT = mybir.ActivationFunctionType
+MULT = mybir.AluOpType.mult
+
+P = 128
+PACK = 4
+PASSES = K // (P * PACK)
+BANK = 512
+HALVES = S // BANK
+N_TILES = N // P
+CHUNK = 512
+CHUNKS = T2 // CHUNK
+
+
+def tile_list_passport_lane_features_kernel(
+    tc, tab_words, tab_scales, offs, offs2, offs3, w1, base, wgs, page0, w2, w3_words, w3_scales,
+    out_0, out_1, out_2, out_3,
+):
+    nc = tc.nc
+    with ExitStack() as ctx:
+        lists = ctx.enter_context(tc.tile_pool(name="lists", bufs=1))
+        keep = ctx.enter_context(tc.tile_pool(name="keep", bufs=1))
+        ring = ctx.enter_context(tc.tile_pool(name="ring", bufs=4))
+        psum = ctx.enter_context(tc.psum_pool(name="psum", bufs=8))
+
+        def half(h):
+            return slice(h * BANK, (h + 1) * BANK)
+
+        def list_half(h):
+            return slice(h * BANK // 16, (h + 1) * BANK // 16)
+
+        pick = lists.tile([P, S // 16], U16, name="pick")
+        put = lists.tile([P, S // 16], U16, name="put")
+        read = lists.tile([P, S // 16], U16, name="read")
+        table = [keep.tile([P, T], I32, name=f"table{a}", tag=f"table{a}", align_bytes=64) for a in range(PASSES)]
+        table_scales = keep.tile([P, T], U8, name="table_scales", align_bytes=64)
+        v_scales = keep.tile([P, S], U8, name="v_scales", align_bytes=64)
+        v_scales_moved = keep.tile([P, (PASSES - 1) * S], U8, name="v_scales_moved", tag="planes_x", align_bytes=64)
+        w1_raw = [keep.tile([P, PACK, H], F32, name=f"w1_raw{a}", tag=f"w1_raw_caps{a}") for a in range(PASSES)]
+        base_rows = keep.tile([P, PACK], F32, name="base_rows")
+        minus_base = keep.tile([P, PACK], F32, name="minus_base")
+        gain_cuts = (0, BANK, 2 * S, PACK * S)
+        gain_parts = [
+            keep.tile([P, gain_cuts[i + 1] - gain_cuts[i]], F32, name=f"gain_part{i}") for i in range(3)
+        ]
+
+        def gains(t, lo, hi):
+            first = t * S + lo
+            i = max(i for i in range(3) if gain_cuts[i] <= first)
+            return gain_parts[i][:, first - gain_cuts[i] : t * S + hi - gain_cuts[i]]
+
+        page = [keep.tile([P, T2], F32, name=f"page{t}") for t in range(PACK)]
+        w2_raw = keep.tile([P, PACK, N], F32, name="w2_raw")
+        w3_codes = keep.tile([P, PASSES, 2 * N], U8, name="w3_codes", tag="w3_w2", align_bytes=64)
+        w3_planes = keep.tile([P, PASSES, N], U8, name="w3_planes", align_bytes=64)
+
+        nc.vector.memset(table_scales[:].bitcast(I32), 0)
+        nc.vector.memset(w3_planes[:].rearrange("p a n -> p (a n)").bitcast(I32), 0)
+        nc.vector.memset(v_scales_moved[:].bitcast(I32), 0)
+
+        def load_table(a):
+            nc.sync.dma_start(out=table[a][:], in_=tab_words[a].rearrange("p t i -> p (t i)").bitcast(I32))
+
+        def load_w1(a):
+            rows = w1[a * P * PACK : (a + 1) * P * PACK, :]
+            nc.sync.dma_start(out=w1_raw[a][:], in_=rows.rearrange("(p j) c -> p j c", j=PACK))
+
+        page_rows = page0.rearrange("(p t) m -> p t m", t=PACK)
+        gain_rows = wgs.rearrange("(i t) j -> i (t j)", t=PACK)
+
+        def load_gains(i):
+            for q in range(4):
+                nc.sync.dma_start(
+                    out=gain_parts[i][32 * q : 32 * q + 32, :], in_=gain_rows[:, gain_cuts[i] : gain_cuts[i + 1]]
+                )
+
+
+        scale_rows = keep.tile([P, T // 4], I32, name="scale_rows")
+        load_table(0)
+        nc.sync.dma_start(pick[:], offs)
+        for q in range(4):
+            nc.sync.dma_start(
+                out=scale_rows[32 * q : 32 * q + 4 * PASSES, :],
+                in_=tab_scales[:, 4 * q : 4 * q + 4, :].bitcast(I32),
+            )
+        nc.scalar.dma_start(out=base_rows[:], in_=base.rearrange("(p t) -> p t", t=PACK))
+        load_w1(0)
+        load_w1(1)
+        load_table(1)
+        load_w1(2)
+        load_table(2)
+        nc.sync.dma_start(put[:], offs2)
+        load_gains(0)
+        nc.sync.dma_start(out=page[0][:], in_=page_rows[:, 0, :])
+
+        shared = {(0, 1): "stage1", (2, 0): "odd"}
+        w1_grouped = {
+            (a, u): keep.tile(
+                [P, PACK * H // 2], BF16, name=f"w1_grouped{a}{u}", tag=shared.get((a, u), f"w1_grouped{a}{u}"), align_bytes=64
+            )
+            for a in range(PASSES)
+            for u in range(2)
+        }
+        v_codes = [
+            keep.tile([P, S], U32, name=f"v_codes{a}", tag=("stage0", "stage1", "odd")[a], align_bytes=64)
+            for a in range(PASSES)
+        ]
+        w1_codes = [keep.tile([P, H], U32, name=f"w1_codes{a}", align_bytes=64) for a in range(PASSES)]
+        w1_scales = [keep.tile([P, H], U8, name=f"w1_scales{a}", align_bytes=64) for a in range(PASSES)]
+
+        def quantize_w1(a, u):
+            nc.scalar.copy(
+                out=w1_grouped[a, u][:].rearrange("p (t m j) -> p m j t", t=2, j=PACK),
+                in_=w1_raw[a][:].rearrange("p j (m t) -> p m j t", t=PACK)[:, :, :, 2 * u : 2 * u + 2],
+            )
+            cols = slice(u * H // 2, (u + 1) * H // 2)
+            nc.vector.quantize_mx(
+                out=w1_codes[a][:, cols].bitcast(FP8X4), scales=w1_scales[a][:, cols], in_=w1_grouped[a, u][:]
+            )
+
+        nc.scalar.activation(out=minus_base[:], in_=base_rows[:], func=ACT.Copy, scale=-1.0)
+        nc.vector.tensor_copy(v_codes[0][:], table[0][:].bitcast(U32).indirect(pick[:]))
+        for q in range(4):
+            rows = slice(32 * q, 32 * q + 4 * PASSES)
+            nc.vector.tensor_copy(table_scales[rows, :].bitcast(I32), scale_rows[rows, :])
+        nc.vector.tensor_copy(v_scales[:], table_scales[:].indirect(pick[:]))
+        quantize_w1(0, 0)
+        quantize_w1(0, 1)
+        nc.vector.tensor_copy(v_codes[1][:], table[1][:].bitcast(U32).indirect(pick[:]))
+        quantize_w1(1, 0)
+        quantize_w1(1, 1)
+        quantize_w1(2, 0)
+        for h in range(HALVES):
+            nc.vector.tensor_copy(v_codes[2][:, half(h)], table[2][:].bitcast(U32).indirect(pick[:, list_half(h)]))
+        quantize_w1(2, 1)
+
+        load_gains(1)
+        nc.sync.dma_start(
+            out=w3_codes[:].bitcast(I32), in_=w3_words.rearrange("a p c -> p a c").bitcast(I32)
+        )
+        for q in range(4):
+            nc.sync.dma_start(
+                out=w3_planes[32 * q : 32 * q + 4, :, :].bitcast(I32),
+                in_=w3_scales[:, 4 * q : 4 * q + 4, :].rearrange("a r n -> r a n").bitcast(I32),
+            )
+        for a in range(1, PASSES):
+            nc.sync.dma_start(
+                out=v_scales_moved[0:112, (a - 1) * S : a * S].bitcast(I32),
+                in_=v_scales[4 * a : 4 * a + 112, :].bitcast(I32),
+            )
+        nc.sync.dma_start(out=page[1][:], in_=page_rows[:, 1, :])
+        load_gains(2)
+        nc.sync.dma_start(out=page[2][:], in_=page_rows[:, 2, :])
+        nc.sync.dma_start(out=w2_raw[:], in_=w2.rearrange("(p j) n -> p j n", j=PACK))
+        nc.sync.dma_start(out=page[3][:], in_=page_rows[:, 3, :])
+        nc.sync.dma_start(read[:], offs3)
+
+        h_rows = [keep.tile([P, S], F32, name=f"h_rows{t}", tag=f"h_page{t}", align_bytes=64) for t in range(PACK)]
+        for t in range(PACK):
+            for h in range(HALVES):
+                acc = psum.tile([P, BANK], F32, name="acc")
+                for a in range(PASSES):
+                    nc.tensor.matmul_mx(
+                        out=acc[:],
+                        lhsT=w1_codes[a][:, t * P : (t + 1) * P].bitcast(FP8X4),
+                        lhsT_scale=w1_scales[a][:, t * P : (t + 1) * P],
+                        rhs=v_codes[a][:, half(h)].bitcast(FP8X4),
+                        rhs_scale=v_scales[4 * a : P, half(h)],
+                        start=(a == 0),
+                        stop=(a == PASSES - 1),
+                    )
+                nc.scalar.activation(
+                    out=h_rows[t][:, half(h)], in_=acc[:], func=ACT.Identity, bias=minus_base[:, t : t + 1]
+                )
+
+        caps = [keep.tile([P, 2, S], F32, name=f"caps{i}", tag=f"w1_raw_caps{i}") for i in range(N_TILES // 2)]
+        for n in range(N_TILES):
+            for h in range(HALVES):
+                acc = psum.tile([P, BANK], F32, name="acc")
+                for a in range(PASSES):
+                    if a == 0:
+                        plane = v_scales[:, half(h)]
+                    else:
+                        plane = v_scales_moved[:, (a - 1) * S + h * BANK : (a - 1) * S + (h + 1) * BANK]
+                    nc.tensor.matmul_mx(
+                        out=acc[:],
+                        lhsT=w3_codes[:, a, 2 * n * P : 2 * (n + 1) * P].bitcast(FP4X4),
+                        lhsT_scale=w3_planes[:, a, n * P : (n + 1) * P],
+                        rhs=v_codes[a][:, half(h)].bitcast(FP8X4),
+                        rhs_scale=plane,
+                        start=(a == 0),
+                        stop=(a == PASSES - 1),
+                    )
+                nc.scalar.copy(out=caps[n // 2][:, n % 2, half(h)], in_=acc[:])
+
+        w2_grouped = keep.tile([P, N * PACK], BF16, name="w2_grouped", tag="w3_w2", align_bytes=64)
+        w2_scales = keep.tile([P, N], U8, name="w2_scales", align_bytes=64)
+        nc.scalar.copy(
+            out=w2_grouped[:].rearrange("p (c i t) -> p c t i", i=4, t=PACK),
+            in_=w2_raw[:].rearrange("p t (c i) -> p c t i", i=4),
+        )
+
+        out_rows = out_1.rearrange("(p t) m -> p t m", t=PACK)
+        page_bf16 = [
+            keep.tile([P, PACK, T2 // 2], BF16, name=f"page_bf16_{u}", tag=f"stage{u}", align_bytes=64) for u in range(2)
+        ]
+        for t in range(PACK):
+            if t == 0:
+                for h in range(HALVES):
+                    nc.vector.tensor_tensor(
+                        page[t][:].indirect(put[:, list_half(h)]), h_rows[t][:, half(h)], gains(t, h * BANK, (h + 1) * BANK), MULT
+                    )
+            else:
+                nc.vector.tensor_tensor(page[t][:].indirect(put[:]), h_rows[t][:], gains(t, 0, S), MULT)
+            nc.sync.dma_start(out=out_rows[:, t, :], in_=page[t][:])
+            for u in range(2):
+                nc.scalar.copy(out=page_bf16[u][:, t, :], in_=page[t][:, u * T2 // 2 : (u + 1) * T2 // 2])
+
+        w2_codes = keep.tile([P, N], U32, name="w2_codes", align_bytes=64)
+
+        def quantize_w2():
+            for lo, hi in ((0, 512), (512, N)):
+                nc.vector.quantize_mx(
+                    out=w2_codes[:, lo:hi].bitcast(FP8X4),
+                    scales=w2_scales[:, lo:hi],
+                    in_=w2_grouped[:, PACK * lo : PACK * hi],
+                )
+
+        page_grouped = [
+            keep.tile([P, CHUNK * PACK], BF16, name=f"page_grouped{c}", tag=f"h_page{c}", align_bytes=64) for c in range(CHUNKS)
+        ]
+        page_codes = keep.tile([P, T2], I32, name="page_codes", align_bytes=64)
+        page_scales = keep.tile([P, T2], U8, name="page_scales", align_bytes=64)
+
+        def finish_chunk(c):
+            cols = slice(c % 2 * CHUNK, (c % 2 + 1) * CHUNK)
+            nc.scalar.copy(
+                out=page_grouped[c][:].rearrange("p (c i t) -> p c t i", i=4, t=PACK),
+                in_=page_bf16[c // 2][:, :, cols].rearrange("p t (c i) -> p c t i", i=4),
+            )
+
+        def quantize_chunk(c):
+            cols = slice(c * CHUNK, (c + 1) * CHUNK)
+            nc.vector.quantize_mx(out=page_codes[:, cols].bitcast(FP8X4), scales=page_scales[:, cols], in_=page_grouped[c][:])
+            nc.sync.dma_start(
+                out=out_2[0].rearrange("p m t -> p (m t)").bitcast(I32)[:, cols], in_=page_codes[:, cols]
+            )
+
+        x_raw = [
+            keep.tile([P, PACK, BANK], F32, name="x_raw0", tag="odd", align_bytes=64),
+            keep.tile([P, PACK, BANK], F32, name="x_raw1", tag="planes_x", align_bytes=64),
+        ]
+        x_grouped = [keep.tile([P, BANK * PACK], BF16, name=f"x_grouped{h}", align_bytes=64) for h in range(HALVES)]
+        x_codes = [keep.tile([P, BANK], U32, name=f"x_codes{h}", align_bytes=64) for h in range(HALVES)]
+        x_scales = [keep.tile([P, BANK], U8, name=f"x_scales{h}", align_bytes=64) for h in range(HALVES)]
+
+        def gather_x(h):
+            for t in range(PACK):
+                nc.vector.tensor_copy(x_raw[h][:, t, :], page[t][:].indirect(read[:, list_half(h)]))
+
+        def group_x(h):
+            nc.scalar.activation(
+                out=x_grouped[h][:].rearrange("p (c i t) -> p c t i", i=4, t=PACK),
+                in_=x_raw[h][:].rearrange("p t (c i) -> p c t i", i=4),
+                func=ACT.Abs,
+            )
+
+        def quantize_x(h):
+            nc.vector.quantize_mx(out=x_codes[h][:].bitcast(FP8X4), scales=x_scales[h][:], in_=x_grouped[h][:])
+
+        def products(h):
+            for n in range(N_TILES):
+                acc = psum.tile([P, BANK], F32, name="acc")
+                nc.tensor.matmul_mx(
+                    out=acc[:],
+                    lhsT=w2_codes[:, n * P : (n + 1) * P].bitcast(FP8X4),
+                    lhsT_scale=w2_scales[:, n * P : (n + 1) * P],
+                    rhs=x_codes[h][:].bitcast(FP8X4),
+                    rhs_scale=x_scales[h][:],
+                    start=True,
+                    stop=True,
+                )
+                y = ring.tile([P, BANK], F32, name="y")
+                nc.vector.tensor_tensor(y[:], acc[:], caps[n // 2][:, n % 2, half(h)], MULT)
+                nc.sync.dma_start(out=out_0[n * P : (n + 1) * P, half(h)], in_=y[:])
+
+        gather_x(0)
+        gather_x(1)
+        quantize_w2()
+        finish_chunk(0)
+        group_x(0)
+        finish_chunk(1)
+        group_x(1)
+        finish_chunk(2)
+        finish_chunk(3)
+        quantize_chunk(0)
+        quantize_x(0)
+        quantize_chunk(1)
+        products(0)
+        quantize_x(1)
+        quantize_chunk(2)
+        quantize_chunk(3)
+        for q in range(4):
+            nc.sync.dma_start(
+                out=out_3[0, 4 * q : 4 * q + 4, :].bitcast(I32), in_=page_scales[32 * q : 32 * q + 4, :].bitcast(I32)
+            )
+        products(1)

@@ -1,6 +1,7 @@
 from contextlib import ExitStack
 
 import concourse.mybir as mybir
+from concourse.masks import make_identity
 
 K, T, S, H, N, T2 = 1536, 2048, 1024, 512, 768, 2048
 FLOPS = 2 * S * (K * H + H * N + K * N)
@@ -22,8 +23,11 @@ PASSES = K // (P * PACK)
 BANK = 512
 HALVES = S // BANK
 N_TILES = N // P
-CHUNK = 512
-CHUNKS = T2 // CHUNK
+ROW_TILES = H // P
+CHUNKS = T2 // BANK
+BLOCKS = BANK // P
+TURN_BANKS = 4
+SUM_BANKS = 4
 
 
 def tile_list_passport_lane_features_kernel(
@@ -35,7 +39,11 @@ def tile_list_passport_lane_features_kernel(
         lists = ctx.enter_context(tc.tile_pool(name="lists", bufs=1))
         keep = ctx.enter_context(tc.tile_pool(name="keep", bufs=1))
         ring = ctx.enter_context(tc.tile_pool(name="ring", bufs=4))
-        psum = ctx.enter_context(tc.psum_pool(name="psum", bufs=8))
+        turn = ctx.enter_context(tc.psum_pool(name="turn", bufs=TURN_BANKS))
+        sums = ctx.enter_context(tc.psum_pool(name="sums", bufs=SUM_BANKS))
+
+        def sbuf(name, shape, dtype, slot=None):
+            return keep.tile(shape, dtype, name=name, tag=slot or name, align_bytes=64)
 
         def half(h):
             return slice(h * BANK, (h + 1) * BANK)
@@ -46,50 +54,39 @@ def tile_list_passport_lane_features_kernel(
         pick = lists.tile([P, S // 16], U16, name="pick")
         put = lists.tile([P, S // 16], U16, name="put")
         read = lists.tile([P, S // 16], U16, name="read")
-        table = [keep.tile([P, T], I32, name=f"table{a}", tag=f"table{a}", align_bytes=64) for a in range(PASSES)]
-        table_scales = keep.tile([P, T], U8, name="table_scales", align_bytes=64)
-        v_scales = keep.tile([P, S], U8, name="v_scales", align_bytes=64)
-        v_scales_moved = keep.tile([P, (PASSES - 1) * S], U8, name="v_scales_moved", tag="planes_x", align_bytes=64)
-        w1_raw = [keep.tile([P, PACK, H], F32, name=f"w1_raw{a}", tag=f"w1_raw_caps{a}") for a in range(PASSES)]
-        base_rows = keep.tile([P, PACK], F32, name="base_rows")
-        minus_base = keep.tile([P, PACK], F32, name="minus_base")
-        gain_cuts = (0, BANK, 2 * S, PACK * S)
-        gain_parts = [
-            keep.tile([P, gain_cuts[i + 1] - gain_cuts[i]], F32, name=f"gain_part{i}") for i in range(3)
-        ]
-
-        def gains(t, lo, hi):
-            first = t * S + lo
-            i = max(i for i in range(3) if gain_cuts[i] <= first)
-            return gain_parts[i][:, first - gain_cuts[i] : t * S + hi - gain_cuts[i]]
-
-        page = [keep.tile([P, T2], F32, name=f"page{t}") for t in range(PACK)]
-        w2_raw = keep.tile([P, PACK, N], F32, name="w2_raw")
-        w3_codes = keep.tile([P, PASSES, 2 * N], U8, name="w3_codes", tag="w3_w2", align_bytes=64)
-        w3_planes = keep.tile([P, PASSES, N], U8, name="w3_planes", align_bytes=64)
+        table = [sbuf(f"table{a}", [P, T], I32) for a in range(PASSES)]
+        scale_rows = sbuf("scale_rows", [P, T // 4], I32)
+        table_scales = sbuf("table_scales", [P, T], U8)
+        v_scales = sbuf("v_scales", [P, S], U8)
+        v_scales_moved = sbuf("v_scales_moved", [P, (PASSES - 1) * S], U8)
+        w1_raw = [sbuf(f"w1_raw{i}", [P, PASSES, PACK, 2 * P], F32) for i in range(ROW_TILES // 2)]
+        base_rows = sbuf("base_rows", [P, ROW_TILES], F32)
+        minus_base = sbuf("minus_base", [P, ROW_TILES], F32)
+        gains = sbuf("gains", [P, S], F32)
+        page = [sbuf(f"page{b}", [P, T2], F32) for b in range(ROW_TILES)]
+        w2_raw = sbuf("w2_raw", [P, PACK, N], F32)
+        w3_codes = sbuf("w3_codes", [P, PASSES, 2 * N], U8)
+        w3_planes = sbuf("w3_planes", [P, PASSES, N], U8)
+        identity = sbuf("identity", [P, P], F32)
 
         nc.vector.memset(table_scales[:].bitcast(I32), 0)
         nc.vector.memset(w3_planes[:].rearrange("p a n -> p (a n)").bitcast(I32), 0)
         nc.vector.memset(v_scales_moved[:].bitcast(I32), 0)
+        make_identity(nc, identity[:])
 
         def load_table(a):
             nc.sync.dma_start(out=table[a][:], in_=tab_words[a].rearrange("p t i -> p (t i)").bitcast(I32))
 
-        def load_w1(a):
-            rows = w1[a * P * PACK : (a + 1) * P * PACK, :]
-            nc.sync.dma_start(out=w1_raw[a][:], in_=rows.rearrange("(p j) c -> p j c", j=PACK))
+        def load_w1(i):
+            for a in range(PASSES):
+                rows = w1[a * P * PACK : (a + 1) * P * PACK, 2 * i * P : 2 * (i + 1) * P]
+                nc.sync.dma_start(out=w1_raw[i][:, a, :, :], in_=rows.rearrange("(p j) c -> p j c", j=PACK))
 
-        page_rows = page0.rearrange("(p t) m -> p t m", t=PACK)
-        gain_rows = wgs.rearrange("(i t) j -> i (t j)", t=PACK)
+        def load_page(b):
+            nc.sync.dma_start(out=page[b][:], in_=page0[b * P : (b + 1) * P, :])
 
-        def load_gains(i):
-            for q in range(4):
-                nc.sync.dma_start(
-                    out=gain_parts[i][32 * q : 32 * q + 32, :], in_=gain_rows[:, gain_cuts[i] : gain_cuts[i + 1]]
-                )
-
-
-        scale_rows = keep.tile([P, T // 4], I32, name="scale_rows")
+        with nc.allow_non_contiguous_dma(reason="one base value for each partition and row tile"):
+            nc.scalar.dma_start(out=base_rows[:], in_=base.rearrange("(b p) -> p b", p=P))
         load_table(0)
         nc.sync.dma_start(pick[:], offs)
         for q in range(4):
@@ -97,61 +94,52 @@ def tile_list_passport_lane_features_kernel(
                 out=scale_rows[32 * q : 32 * q + 4 * PASSES, :],
                 in_=tab_scales[:, 4 * q : 4 * q + 4, :].bitcast(I32),
             )
-        nc.scalar.dma_start(out=base_rows[:], in_=base.rearrange("(p t) -> p t", t=PACK))
         load_w1(0)
-        load_w1(1)
         load_table(1)
-        load_w1(2)
         load_table(2)
         nc.sync.dma_start(put[:], offs2)
-        load_gains(0)
-        nc.sync.dma_start(out=page[0][:], in_=page_rows[:, 0, :])
+        nc.sync.dma_start(out=gains[:], in_=wgs)
+        load_page(0)
 
-        shared = {(0, 1): "stage1", (2, 0): "odd"}
-        w1_grouped = {
-            (a, u): keep.tile(
-                [P, PACK * H // 2], BF16, name=f"w1_grouped{a}{u}", tag=shared.get((a, u), f"w1_grouped{a}{u}"), align_bytes=64
-            )
-            for a in range(PASSES)
-            for u in range(2)
-        }
-        v_codes = [
-            keep.tile([P, S], U32, name=f"v_codes{a}", tag=("stage0", "stage1", "odd")[a], align_bytes=64)
-            for a in range(PASSES)
-        ]
-        w1_codes = [keep.tile([P, H], U32, name=f"w1_codes{a}", align_bytes=64) for a in range(PASSES)]
-        w1_scales = [keep.tile([P, H], U8, name=f"w1_scales{a}", align_bytes=64) for a in range(PASSES)]
+        w1_grouped = [sbuf(f"w1_grouped{b}", [P, PASSES * P * PACK], BF16) for b in range(ROW_TILES)]
+        w1_scales = [sbuf(f"w1_scales{b}", [P, PASSES * P], U8) for b in range(ROW_TILES)]
+        w1_codes = {}
+        h_rows = {}
 
-        def quantize_w1(a, u):
+        def interleave(out, in_):
             nc.scalar.copy(
-                out=w1_grouped[a, u][:].rearrange("p (t m j) -> p m j t", t=2, j=PACK),
-                in_=w1_raw[a][:].rearrange("p j (m t) -> p m j t", t=PACK)[:, :, :, 2 * u : 2 * u + 2],
+                out=out.rearrange("p (c i t) -> p c t i", i=4, t=PACK), in_=in_.rearrange("p t (c i) -> p c t i", i=4)
             )
-            cols = slice(u * H // 2, (u + 1) * H // 2)
-            nc.vector.quantize_mx(
-                out=w1_codes[a][:, cols].bitcast(FP8X4), scales=w1_scales[a][:, cols], in_=w1_grouped[a, u][:]
-            )
+
+        def group_w1(b):
+            for a in range(PASSES):
+                interleave(w1_grouped[b][:, a * P * PACK : (a + 1) * P * PACK], w1_raw[b // 2][:, a, :, b % 2 * P : (b % 2 + 1) * P])
+
+        def quantize_w1(b):
+            w1_codes[b] = sbuf(f"w1_codes{b}", [P, PASSES * P], U32, "table2" if b == 1 else None)
+            for a in range(PASSES):
+                cols = slice(a * P, (a + 1) * P)
+                nc.vector.quantize_mx(
+                    out=w1_codes[b][:, cols].bitcast(FP8X4),
+                    scales=w1_scales[b][:, cols],
+                    in_=w1_grouped[b][:, a * P * PACK : (a + 1) * P * PACK],
+                )
 
         nc.scalar.activation(out=minus_base[:], in_=base_rows[:], func=ACT.Copy, scale=-1.0)
+        v_codes = [sbuf(f"v_codes{a}", [P, S], U32) for a in range(PASSES - 1)]
         nc.vector.tensor_copy(v_codes[0][:], table[0][:].bitcast(U32).indirect(pick[:]))
         for q in range(4):
             rows = slice(32 * q, 32 * q + 4 * PASSES)
             nc.vector.tensor_copy(table_scales[rows, :].bitcast(I32), scale_rows[rows, :])
         nc.vector.tensor_copy(v_scales[:], table_scales[:].indirect(pick[:]))
-        quantize_w1(0, 0)
-        quantize_w1(0, 1)
+        group_w1(0)
+        quantize_w1(0)
         nc.vector.tensor_copy(v_codes[1][:], table[1][:].bitcast(U32).indirect(pick[:]))
-        quantize_w1(1, 0)
-        quantize_w1(1, 1)
-        quantize_w1(2, 0)
+        v_codes.append(sbuf("v_codes2", [P, S], U32, "w1_grouped0"))
         for h in range(HALVES):
             nc.vector.tensor_copy(v_codes[2][:, half(h)], table[2][:].bitcast(U32).indirect(pick[:, list_half(h)]))
-        quantize_w1(2, 1)
 
-        load_gains(1)
-        nc.sync.dma_start(
-            out=w3_codes[:].bitcast(I32), in_=w3_words.rearrange("a p c -> p a c").bitcast(I32)
-        )
+        nc.sync.dma_start(out=w3_codes[:].bitcast(I32), in_=w3_words.rearrange("a p c -> p a c").bitcast(I32))
         for q in range(4):
             nc.sync.dma_start(
                 out=w3_planes[32 * q : 32 * q + 4, :, :].bitcast(I32),
@@ -162,35 +150,94 @@ def tile_list_passport_lane_features_kernel(
                 out=v_scales_moved[0:112, (a - 1) * S : a * S].bitcast(I32),
                 in_=v_scales[4 * a : 4 * a + 112, :].bitcast(I32),
             )
-        nc.sync.dma_start(out=page[1][:], in_=page_rows[:, 1, :])
-        load_gains(2)
-        nc.sync.dma_start(out=page[2][:], in_=page_rows[:, 2, :])
-        nc.sync.dma_start(out=w2_raw[:], in_=w2.rearrange("(p j) n -> p j n", j=PACK))
-        nc.sync.dma_start(out=page[3][:], in_=page_rows[:, 3, :])
+        load_page(1)
+        load_w1(1)
         nc.sync.dma_start(read[:], offs3)
+        nc.sync.dma_start(out=w2_raw[:], in_=w2.rearrange("(p j) n -> p j n", j=PACK))
+        load_page(2)
+        load_page(3)
 
-        h_rows = [keep.tile([P, S], F32, name=f"h_rows{t}", tag=f"h_page{t}", align_bytes=64) for t in range(PACK)]
-        for t in range(PACK):
+        def make_h(b):
+            h_rows[b] = sbuf(f"h_rows{b}", [P, S], F32)
             for h in range(HALVES):
-                acc = psum.tile([P, BANK], F32, name="acc")
+                bank = turn.tile([P, BANK], F32, name="bank")
                 for a in range(PASSES):
                     nc.tensor.matmul_mx(
-                        out=acc[:],
-                        lhsT=w1_codes[a][:, t * P : (t + 1) * P].bitcast(FP8X4),
-                        lhsT_scale=w1_scales[a][:, t * P : (t + 1) * P],
+                        out=bank[:],
+                        lhsT=w1_codes[b][:, a * P : (a + 1) * P].bitcast(FP8X4),
+                        lhsT_scale=w1_scales[b][:, a * P : (a + 1) * P],
                         rhs=v_codes[a][:, half(h)].bitcast(FP8X4),
                         rhs_scale=v_scales[4 * a : P, half(h)],
                         start=(a == 0),
                         stop=(a == PASSES - 1),
                     )
                 nc.scalar.activation(
-                    out=h_rows[t][:, half(h)], in_=acc[:], func=ACT.Identity, bias=minus_base[:, t : t + 1]
+                    out=h_rows[b][:, half(h)], in_=bank[:], func=ACT.Identity, bias=minus_base[:, b : b + 1]
                 )
 
-        caps = [keep.tile([P, 2, S], F32, name=f"caps{i}", tag=f"w1_raw_caps{i}") for i in range(N_TILES // 2)]
+        def scatter(b, lo, hi):
+            window = page[b][:].indirect(put[:, lo // 16 : hi // 16])
+            nc.vector.tensor_tensor(window, h_rows[b][:, lo:hi], gains[:, lo:hi], MULT)
+
+        def turn_rows(source, turned, b, absolute):
+            bank = turn.tile([P, BANK], F32, name="bank")
+            for g in range(BLOCKS):
+                nc.tensor.transpose(bank[:, g * P : (g + 1) * P], source[:, g * P : (g + 1) * P], identity[:])
+            out = turned[:].rearrange("m (g u b i e) -> m g u b i e", g=BLOCKS, u=2, b=ROW_TILES, e=2)[:, :, :, b, :, :]
+            in_ = bank[:].rearrange("m (g i u e) -> m g u i e", g=BLOCKS, u=2, e=2)
+            if absolute:
+                for u in range(2):
+                    nc.scalar.activation(out=out[:, :, u, :, :], in_=in_[:, :, u, :, :], func=ACT.Abs)
+            else:
+                nc.scalar.copy(out=out, in_=in_)
+
+        def turn_back(turned, grouped):
+            for k in range(2):
+                bank = turn.tile([P, BANK], F32, name="bank")
+                for s in range(BLOCKS):
+                    first = k * BANK + s * P
+                    nc.tensor.transpose(
+                        bank[:, s * P : (s + 1) * P], turned[:].bitcast(F32)[:, first : first + P], identity[:]
+                    )
+                nc.scalar.copy(
+                    out=grouped[:].bitcast(F32)[:, half(k)].rearrange("p (g m u) -> p g m u", g=2, u=2),
+                    in_=bank[:].rearrange("p (g u m) -> p g m u", g=2, u=2),
+                )
+
+        page_turned = [sbuf(f"page_turned{c}", [P, BLOCKS * H], BF16) for c in range(CHUNKS)]
+        x_turned = [sbuf(f"x_turned{h}", [P, BLOCKS * H], BF16) for h in range(HALVES)]
+        x_raw = {}
+
+        def gather_x(b, lo, hi):
+            nc.vector.tensor_copy(x_raw[b][:, lo:hi], page[b][:].indirect(read[:, lo // 16 : hi // 16]))
+
+        def turn_page(b, c):
+            turn_rows(page[b][:, half(c)], page_turned[c], b, False)
+
+        def turn_x(b, h):
+            turn_rows(x_raw[b][:, half(h)], x_turned[h], b, True)
+
+        def store_page(b):
+            nc.sync.dma_start(out=out_1[b * P : (b + 1) * P, :], in_=page[b][:])
+
+        last = ROW_TILES - 1
+        make_h(0)
+        group_w1(1)
+        quantize_w1(1)
+        make_h(1)
+        scatter(0, 0, BANK)
+        scatter(0, BANK, S)
+        store_page(0)
+        scatter(1, 0, S)
+        store_page(1)
+        for b in (2, 3):
+            group_w1(b)
+            quantize_w1(b)
+
+        caps = [sbuf(f"caps{i}", [P, 2, S], F32, f"table{i}") for i in range(N_TILES // 2)]
         for n in range(N_TILES):
             for h in range(HALVES):
-                acc = psum.tile([P, BANK], F32, name="acc")
+                acc = turn.tile([P, BANK], F32, name="bank")
                 for a in range(PASSES):
                     if a == 0:
                         plane = v_scales[:, half(h)]
@@ -207,84 +254,61 @@ def tile_list_passport_lane_features_kernel(
                     )
                 nc.scalar.copy(out=caps[n // 2][:, n % 2, half(h)], in_=acc[:])
 
-        w2_grouped = keep.tile([P, N * PACK], BF16, name="w2_grouped", tag="w3_w2", align_bytes=64)
-        w2_scales = keep.tile([P, N], U8, name="w2_scales", align_bytes=64)
-        nc.scalar.copy(
-            out=w2_grouped[:].rearrange("p (c i t) -> p c t i", i=4, t=PACK),
-            in_=w2_raw[:].rearrange("p t (c i) -> p c t i", i=4),
-        )
+        make_h(2)
+        make_h(3)
+        w2_grouped = sbuf("w2_grouped", [P, N * PACK], BF16, f"w1_codes{last}")
+        for lo in range(0, N, 256):
+            interleave(w2_grouped[:, PACK * lo : PACK * (lo + 256)], w2_raw[:, :, lo : lo + 256])
 
-        out_rows = out_1.rearrange("(p t) m -> p t m", t=PACK)
-        page_bf16 = [
-            keep.tile([P, PACK, T2 // 2], BF16, name=f"page_bf16_{u}", tag=f"stage{u}", align_bytes=64) for u in range(2)
-        ]
-        for t in range(PACK):
-            if t == 0:
+        x_raw[0] = sbuf("x_raw0", [P, S], F32, f"w1_grouped{last}")
+        gather_x(0, 0, S)
+        scatter(2, 0, S)
+        store_page(2)
+        x_raw[1] = sbuf("x_raw1", [P, S], F32, "h_rows2")
+        gather_x(1, 0, S)
+        scatter(last, 0, S)
+        store_page(last)
+        x_raw[2] = sbuf("x_raw2", [P, S], F32, f"h_rows{last}")
+        for b in range(last):
+            for c in range(CHUNKS):
+                turn_page(b, c)
+            if b > 0:
                 for h in range(HALVES):
-                    nc.vector.tensor_tensor(
-                        page[t][:].indirect(put[:, list_half(h)]), h_rows[t][:, half(h)], gains(t, h * BANK, (h + 1) * BANK), MULT
-                    )
-            else:
-                nc.vector.tensor_tensor(page[t][:].indirect(put[:]), h_rows[t][:], gains(t, 0, S), MULT)
-            nc.sync.dma_start(out=out_rows[:, t, :], in_=page[t][:])
-            for u in range(2):
-                nc.scalar.copy(out=page_bf16[u][:, t, :], in_=page[t][:, u * T2 // 2 : (u + 1) * T2 // 2])
+                    turn_x(b - 1, h)
 
-        w2_codes = keep.tile([P, N], U32, name="w2_codes", align_bytes=64)
+        x_raw[last] = sbuf(f"x_raw{last}", [P, S], F32)
+        for h in range(HALVES):
+            for b in (last - 1, last):
+                gather_x(b, h * BANK, (h + 1) * BANK)
 
-        def quantize_w2():
-            for lo, hi in ((0, 512), (512, N)):
-                nc.vector.quantize_mx(
-                    out=w2_codes[:, lo:hi].bitcast(FP8X4),
-                    scales=w2_scales[:, lo:hi],
-                    in_=w2_grouped[:, PACK * lo : PACK * hi],
-                )
-
-        page_grouped = [
-            keep.tile([P, CHUNK * PACK], BF16, name=f"page_grouped{c}", tag=f"h_page{c}", align_bytes=64) for c in range(CHUNKS)
-        ]
-        page_codes = keep.tile([P, T2], I32, name="page_codes", align_bytes=64)
-        page_scales = keep.tile([P, T2], U8, name="page_scales", align_bytes=64)
-
-        def finish_chunk(c):
-            cols = slice(c % 2 * CHUNK, (c % 2 + 1) * CHUNK)
-            nc.scalar.copy(
-                out=page_grouped[c][:].rearrange("p (c i t) -> p c t i", i=4, t=PACK),
-                in_=page_bf16[c // 2][:, :, cols].rearrange("p t (c i) -> p c t i", i=4),
+        w2_codes = sbuf("w2_codes", [P, N], U32, "gains")
+        w2_scales = sbuf("w2_scales", [P, N], U8)
+        for lo, hi in ((0, 512), (512, N)):
+            nc.vector.quantize_mx(
+                out=w2_codes[:, lo:hi].bitcast(FP8X4), scales=w2_scales[:, lo:hi], in_=w2_grouped[:, PACK * lo : PACK * hi]
             )
+
+        page_grouped = [sbuf(f"page_grouped{c}", [P, BANK * PACK], BF16, f"w1_raw{c}" if c < 2 else None) for c in range(CHUNKS)]
+        page_codes = sbuf("page_codes", [P, T2], I32)
+        page_scales = sbuf("page_scales", [P, T2], U8)
+        x_grouped = [sbuf(f"x_grouped{h}", [P, BANK * PACK], BF16) for h in range(HALVES)]
+        x_codes = [sbuf(f"x_codes{h}", [P, BANK], U32) for h in range(HALVES)]
+        x_scales = [sbuf(f"x_scales{h}", [P, BANK], U8) for h in range(HALVES)]
 
         def quantize_chunk(c):
-            cols = slice(c * CHUNK, (c + 1) * CHUNK)
-            nc.vector.quantize_mx(out=page_codes[:, cols].bitcast(FP8X4), scales=page_scales[:, cols], in_=page_grouped[c][:])
-            nc.sync.dma_start(
-                out=out_2[0].rearrange("p m t -> p (m t)").bitcast(I32)[:, cols], in_=page_codes[:, cols]
+            nc.vector.quantize_mx(
+                out=page_codes[:, half(c)].bitcast(FP8X4), scales=page_scales[:, half(c)], in_=page_grouped[c][:]
             )
-
-        x_raw = [
-            keep.tile([P, PACK, BANK], F32, name="x_raw0", tag="odd", align_bytes=64),
-            keep.tile([P, PACK, BANK], F32, name="x_raw1", tag="planes_x", align_bytes=64),
-        ]
-        x_grouped = [keep.tile([P, BANK * PACK], BF16, name=f"x_grouped{h}", align_bytes=64) for h in range(HALVES)]
-        x_codes = [keep.tile([P, BANK], U32, name=f"x_codes{h}", align_bytes=64) for h in range(HALVES)]
-        x_scales = [keep.tile([P, BANK], U8, name=f"x_scales{h}", align_bytes=64) for h in range(HALVES)]
-
-        def gather_x(h):
-            for t in range(PACK):
-                nc.vector.tensor_copy(x_raw[h][:, t, :], page[t][:].indirect(read[:, list_half(h)]))
-
-        def group_x(h):
-            nc.scalar.activation(
-                out=x_grouped[h][:].rearrange("p (c i t) -> p c t i", i=4, t=PACK),
-                in_=x_raw[h][:].rearrange("p t (c i) -> p c t i", i=4),
-                func=ACT.Abs,
+            nc.sync.dma_start(
+                out=out_2[0].rearrange("p m t -> p (m t)").bitcast(I32)[:, half(c)], in_=page_codes[:, half(c)]
             )
 
         def quantize_x(h):
             nc.vector.quantize_mx(out=x_codes[h][:].bitcast(FP8X4), scales=x_scales[h][:], in_=x_grouped[h][:])
 
-        def products(h):
-            for n in range(N_TILES):
-                acc = psum.tile([P, BANK], F32, name="acc")
+        def products(h, tiles):
+            for n in tiles:
+                acc = sums.tile([P, BANK], F32, name="acc")
                 nc.tensor.matmul_mx(
                     out=acc[:],
                     lhsT=w2_codes[:, n * P : (n + 1) * P].bitcast(FP8X4),
@@ -298,24 +322,29 @@ def tile_list_passport_lane_features_kernel(
                 nc.vector.tensor_tensor(y[:], acc[:], caps[n // 2][:, n % 2, half(h)], MULT)
                 nc.sync.dma_start(out=out_0[n * P : (n + 1) * P, half(h)], in_=y[:])
 
-        gather_x(0)
-        gather_x(1)
-        quantize_w2()
-        finish_chunk(0)
-        group_x(0)
-        finish_chunk(1)
-        group_x(1)
-        finish_chunk(2)
-        finish_chunk(3)
-        quantize_chunk(0)
+        turn_page(last, 0)
+        turn_x(last - 1, 0)
+        turn_page(last, 1)
+        turn_x(last, 0)
+        turn_back(x_turned[0], x_grouped[0])
         quantize_x(0)
-        quantize_chunk(1)
-        products(0)
+        products(0, range(N_TILES))
+        turn_x(last - 1, 1)
+        turn_x(last, 1)
+        turn_back(x_turned[1], x_grouped[1])
         quantize_x(1)
+        for c in range(CHUNKS):
+            if c >= 2:
+                turn_page(last, c)
+            turn_back(page_turned[c], page_grouped[c])
+        quantize_chunk(0)
+        products(1, range(0, 2))
+        quantize_chunk(1)
+        products(1, range(2, 4))
         quantize_chunk(2)
         quantize_chunk(3)
         for q in range(4):
             nc.sync.dma_start(
                 out=out_3[0, 4 * q : 4 * q + 4, :].bitcast(I32), in_=page_scales[32 * q : 32 * q + 4, :].bitcast(I32)
             )
-        products(1)
+        products(1, range(4, N_TILES))

from contextlib import ExitStack

import concourse.mybir as mybir
from concourse.masks import make_identity

K, T, S, H, N, T2 = 1536, 2048, 1024, 512, 768, 2048
FLOPS = 2 * S * (K * H + H * N + K * N)

F32 = mybir.dt.float32
BF16 = mybir.dt.bfloat16
I32 = mybir.dt.int32
U32 = mybir.dt.uint32
U16 = mybir.dt.uint16
U8 = mybir.dt.uint8
FP8X4 = mybir.dt.float8_e4m3fn_x4
FP4X4 = mybir.dt.float4_e2m1fn_x4
ACT = mybir.ActivationFunctionType
MULT = mybir.AluOpType.mult

P = 128
PACK = 4
PASSES = K // (P * PACK)
BANK = 512
HALVES = S // BANK
N_TILES = N // P
ROW_TILES = H // P
CHUNKS = T2 // BANK
BLOCKS = BANK // P
TURN_BANKS = 4
SUM_BANKS = 4


def tile_list_passport_lane_features_kernel(
    tc, tab_words, tab_scales, offs, offs2, offs3, w1, base, wgs, page0, w2, w3_words, w3_scales,
    out_0, out_1, out_2, out_3,
):
    nc = tc.nc
    with ExitStack() as ctx:
        lists = ctx.enter_context(tc.tile_pool(name="lists", bufs=1))
        keep = ctx.enter_context(tc.tile_pool(name="keep", bufs=1))
        ring = ctx.enter_context(tc.tile_pool(name="ring", bufs=4))
        turn = ctx.enter_context(tc.psum_pool(name="turn", bufs=TURN_BANKS))
        sums = ctx.enter_context(tc.psum_pool(name="sums", bufs=SUM_BANKS))

        def sbuf(name, shape, dtype, slot=None):
            return keep.tile(shape, dtype, name=name, tag=slot or name, align_bytes=64)

        def half(h):
            return slice(h * BANK, (h + 1) * BANK)

        def list_half(h):
            return slice(h * BANK // 16, (h + 1) * BANK // 16)

        pick = lists.tile([P, S // 16], U16, name="pick")
        put = lists.tile([P, S // 16], U16, name="put")
        read = lists.tile([P, S // 16], U16, name="read")
        table = [sbuf(f"table{a}", [P, T], I32) for a in range(PASSES)]
        scale_rows = sbuf("scale_rows", [P, T // 4], I32)
        table_scales = sbuf("table_scales", [P, T], U8)
        v_scales = sbuf("v_scales", [P, S], U8)
        v_scales_moved = sbuf("v_scales_moved", [P, (PASSES - 1) * S], U8)
        w1_raw = [sbuf(f"w1_raw{i}", [P, PASSES, PACK, 2 * P], F32) for i in range(ROW_TILES // 2)]
        base_rows = sbuf("base_rows", [P, ROW_TILES], F32)
        minus_base = sbuf("minus_base", [P, ROW_TILES], F32)
        gains = sbuf("gains", [P, S], F32)
        page = [sbuf(f"page{b}", [P, T2], F32) for b in range(ROW_TILES)]
        w2_raw = sbuf("w2_raw", [P, PACK, N], F32)
        w3_codes = sbuf("w3_codes", [P, PASSES, 2 * N], U8)
        w3_planes = sbuf("w3_planes", [P, PASSES, N], U8)
        identity = sbuf("identity", [P, P], F32)

        nc.vector.memset(table_scales[:].bitcast(I32), 0)
        nc.vector.memset(w3_planes[:].rearrange("p a n -> p (a n)").bitcast(I32), 0)
        nc.vector.memset(v_scales_moved[:].bitcast(I32), 0)
        make_identity(nc, identity[:])

        def load_table(a):
            nc.sync.dma_start(out=table[a][:], in_=tab_words[a].rearrange("p t i -> p (t i)").bitcast(I32))

        def load_w1(i):
            for a in range(PASSES):
                rows = w1[a * P * PACK : (a + 1) * P * PACK, 2 * i * P : 2 * (i + 1) * P]
                nc.sync.dma_start(out=w1_raw[i][:, a, :, :], in_=rows.rearrange("(p j) c -> p j c", j=PACK))

        def load_page(b):
            nc.sync.dma_start(out=page[b][:], in_=page0[b * P : (b + 1) * P, :])

        with nc.allow_non_contiguous_dma(reason="one base value for each partition and row tile"):
            nc.scalar.dma_start(out=base_rows[:], in_=base.rearrange("(b p) -> p b", p=P))
        load_table(0)
        nc.sync.dma_start(pick[:], offs)
        for q in range(4):
            nc.sync.dma_start(
                out=scale_rows[32 * q : 32 * q + 4 * PASSES, :],
                in_=tab_scales[:, 4 * q : 4 * q + 4, :].bitcast(I32),
            )
        load_w1(0)
        load_table(1)
        load_table(2)
        nc.sync.dma_start(put[:], offs2)
        nc.sync.dma_start(out=gains[:], in_=wgs)
        load_page(0)

        w1_grouped = [sbuf(f"w1_grouped{b}", [P, PASSES * P * PACK], BF16) for b in range(ROW_TILES)]
        w1_scales = [sbuf(f"w1_scales{b}", [P, PASSES * P], U8) for b in range(ROW_TILES)]
        w1_codes = {}
        h_rows = {}

        def interleave(out, in_):
            nc.scalar.copy(
                out=out.rearrange("p (c i t) -> p c t i", i=4, t=PACK), in_=in_.rearrange("p t (c i) -> p c t i", i=4)
            )

        def group_w1(b):
            for a in range(PASSES):
                interleave(w1_grouped[b][:, a * P * PACK : (a + 1) * P * PACK], w1_raw[b // 2][:, a, :, b % 2 * P : (b % 2 + 1) * P])

        def quantize_w1(b):
            w1_codes[b] = sbuf(f"w1_codes{b}", [P, PASSES * P], U32, "table2" if b == 1 else None)
            for a in range(PASSES):
                cols = slice(a * P, (a + 1) * P)
                nc.vector.quantize_mx(
                    out=w1_codes[b][:, cols].bitcast(FP8X4),
                    scales=w1_scales[b][:, cols],
                    in_=w1_grouped[b][:, a * P * PACK : (a + 1) * P * PACK],
                )

        nc.scalar.activation(out=minus_base[:], in_=base_rows[:], func=ACT.Copy, scale=-1.0)
        v_codes = [sbuf(f"v_codes{a}", [P, S], U32) for a in range(PASSES - 1)]
        nc.vector.tensor_copy(v_codes[0][:], table[0][:].bitcast(U32).indirect(pick[:]))
        for q in range(4):
            rows = slice(32 * q, 32 * q + 4 * PASSES)
            nc.vector.tensor_copy(table_scales[rows, :].bitcast(I32), scale_rows[rows, :])
        nc.vector.tensor_copy(v_scales[:], table_scales[:].indirect(pick[:]))
        group_w1(0)
        quantize_w1(0)
        nc.vector.tensor_copy(v_codes[1][:], table[1][:].bitcast(U32).indirect(pick[:]))
        v_codes.append(sbuf("v_codes2", [P, S], U32, "w1_grouped0"))
        for h in range(HALVES):
            nc.vector.tensor_copy(v_codes[2][:, half(h)], table[2][:].bitcast(U32).indirect(pick[:, list_half(h)]))

        nc.sync.dma_start(out=w3_codes[:].bitcast(I32), in_=w3_words.rearrange("a p c -> p a c").bitcast(I32))
        for q in range(4):
            nc.sync.dma_start(
                out=w3_planes[32 * q : 32 * q + 4, :, :].bitcast(I32),
                in_=w3_scales[:, 4 * q : 4 * q + 4, :].rearrange("a r n -> r a n").bitcast(I32),
            )
        for a in range(1, PASSES):
            nc.sync.dma_start(
                out=v_scales_moved[0:112, (a - 1) * S : a * S].bitcast(I32),
                in_=v_scales[4 * a : 4 * a + 112, :].bitcast(I32),
            )
        load_page(1)
        load_w1(1)
        nc.sync.dma_start(read[:], offs3)
        nc.sync.dma_start(out=w2_raw[:], in_=w2.rearrange("(p j) n -> p j n", j=PACK))
        load_page(2)
        load_page(3)

        def make_h(b):
            h_rows[b] = sbuf(f"h_rows{b}", [P, S], F32)
            for h in range(HALVES):
                bank = turn.tile([P, BANK], F32, name="bank")
                for a in range(PASSES):
                    nc.tensor.matmul_mx(
                        out=bank[:],
                        lhsT=w1_codes[b][:, a * P : (a + 1) * P].bitcast(FP8X4),
                        lhsT_scale=w1_scales[b][:, a * P : (a + 1) * P],
                        rhs=v_codes[a][:, half(h)].bitcast(FP8X4),
                        rhs_scale=v_scales[4 * a : P, half(h)],
                        start=(a == 0),
                        stop=(a == PASSES - 1),
                    )
                nc.scalar.activation(
                    out=h_rows[b][:, half(h)], in_=bank[:], func=ACT.Identity, bias=minus_base[:, b : b + 1]
                )

        def scatter(b, lo, hi):
            window = page[b][:].indirect(put[:, lo // 16 : hi // 16])
            nc.vector.tensor_tensor(window, h_rows[b][:, lo:hi], gains[:, lo:hi], MULT)

        def turn_rows(source, turned, b, absolute):
            bank = turn.tile([P, BANK], F32, name="bank")
            for g in range(BLOCKS):
                nc.tensor.transpose(bank[:, g * P : (g + 1) * P], source[:, g * P : (g + 1) * P], identity[:])
            out = turned[:].rearrange("m (g u b i e) -> m g u b i e", g=BLOCKS, u=2, b=ROW_TILES, e=2)[:, :, :, b, :, :]
            in_ = bank[:].rearrange("m (g i u e) -> m g u i e", g=BLOCKS, u=2, e=2)
            if absolute:
                for u in range(2):
                    nc.scalar.activation(out=out[:, :, u, :, :], in_=in_[:, :, u, :, :], func=ACT.Abs)
            else:
                nc.scalar.copy(out=out, in_=in_)

        def turn_back(turned, grouped):
            for k in range(2):
                bank = turn.tile([P, BANK], F32, name="bank")
                for s in range(BLOCKS):
                    first = k * BANK + s * P
                    nc.tensor.transpose(
                        bank[:, s * P : (s + 1) * P], turned[:].bitcast(F32)[:, first : first + P], identity[:]
                    )
                nc.scalar.copy(
                    out=grouped[:].bitcast(F32)[:, half(k)].rearrange("p (g m u) -> p g m u", g=2, u=2),
                    in_=bank[:].rearrange("p (g u m) -> p g m u", g=2, u=2),
                )

        page_turned = [sbuf(f"page_turned{c}", [P, BLOCKS * H], BF16) for c in range(CHUNKS)]
        x_turned = [sbuf(f"x_turned{h}", [P, BLOCKS * H], BF16) for h in range(HALVES)]
        x_raw = {}

        def gather_x(b, lo, hi):
            nc.vector.tensor_copy(x_raw[b][:, lo:hi], page[b][:].indirect(read[:, lo // 16 : hi // 16]))

        def turn_page(b, c):
            turn_rows(page[b][:, half(c)], page_turned[c], b, False)

        def turn_x(b, h):
            turn_rows(x_raw[b][:, half(h)], x_turned[h], b, True)

        def store_page(b):
            nc.sync.dma_start(out=out_1[b * P : (b + 1) * P, :], in_=page[b][:])

        last = ROW_TILES - 1
        make_h(0)
        group_w1(1)
        quantize_w1(1)
        make_h(1)
        scatter(0, 0, BANK)
        scatter(0, BANK, S)
        store_page(0)
        scatter(1, 0, S)
        store_page(1)
        for b in (2, 3):
            group_w1(b)
            quantize_w1(b)

        caps = [sbuf(f"caps{i}", [P, 2, S], F32, f"table{i}") for i in range(N_TILES // 2)]
        for n in range(N_TILES):
            for h in range(HALVES):
                acc = turn.tile([P, BANK], F32, name="bank")
                for a in range(PASSES):
                    if a == 0:
                        plane = v_scales[:, half(h)]
                    else:
                        plane = v_scales_moved[:, (a - 1) * S + h * BANK : (a - 1) * S + (h + 1) * BANK]
                    nc.tensor.matmul_mx(
                        out=acc[:],
                        lhsT=w3_codes[:, a, 2 * n * P : 2 * (n + 1) * P].bitcast(FP4X4),
                        lhsT_scale=w3_planes[:, a, n * P : (n + 1) * P],
                        rhs=v_codes[a][:, half(h)].bitcast(FP8X4),
                        rhs_scale=plane,
                        start=(a == 0),
                        stop=(a == PASSES - 1),
                    )
                nc.scalar.copy(out=caps[n // 2][:, n % 2, half(h)], in_=acc[:])

        make_h(2)
        make_h(3)
        w2_grouped = sbuf("w2_grouped", [P, N * PACK], BF16, f"w1_codes{last}")
        for lo in range(0, N, 256):
            interleave(w2_grouped[:, PACK * lo : PACK * (lo + 256)], w2_raw[:, :, lo : lo + 256])

        x_raw[0] = sbuf("x_raw0", [P, S], F32, f"w1_grouped{last}")
        gather_x(0, 0, S)
        scatter(2, 0, S)
        store_page(2)
        x_raw[1] = sbuf("x_raw1", [P, S], F32, "h_rows2")
        gather_x(1, 0, S)
        scatter(last, 0, S)
        store_page(last)
        x_raw[2] = sbuf("x_raw2", [P, S], F32, f"h_rows{last}")
        for b in range(last):
            for c in range(CHUNKS):
                turn_page(b, c)
            if b > 0:
                for h in range(HALVES):
                    turn_x(b - 1, h)

        x_raw[last] = sbuf(f"x_raw{last}", [P, S], F32)
        for h in range(HALVES):
            for b in (last - 1, last):
                gather_x(b, h * BANK, (h + 1) * BANK)

        w2_codes = sbuf("w2_codes", [P, N], U32, "gains")
        w2_scales = sbuf("w2_scales", [P, N], U8)
        for lo, hi in ((0, 512), (512, N)):
            nc.vector.quantize_mx(
                out=w2_codes[:, lo:hi].bitcast(FP8X4), scales=w2_scales[:, lo:hi], in_=w2_grouped[:, PACK * lo : PACK * hi]
            )

        page_grouped = [sbuf(f"page_grouped{c}", [P, BANK * PACK], BF16, f"w1_raw{c}" if c < 2 else None) for c in range(CHUNKS)]
        page_codes = sbuf("page_codes", [P, T2], I32)
        page_scales = sbuf("page_scales", [P, T2], U8)
        x_grouped = [sbuf(f"x_grouped{h}", [P, BANK * PACK], BF16) for h in range(HALVES)]
        x_codes = [sbuf(f"x_codes{h}", [P, BANK], U32) for h in range(HALVES)]
        x_scales = [sbuf(f"x_scales{h}", [P, BANK], U8) for h in range(HALVES)]

        def quantize_chunk(c):
            nc.vector.quantize_mx(
                out=page_codes[:, half(c)].bitcast(FP8X4), scales=page_scales[:, half(c)], in_=page_grouped[c][:]
            )
            nc.sync.dma_start(
                out=out_2[0].rearrange("p m t -> p (m t)").bitcast(I32)[:, half(c)], in_=page_codes[:, half(c)]
            )

        def quantize_x(h):
            nc.vector.quantize_mx(out=x_codes[h][:].bitcast(FP8X4), scales=x_scales[h][:], in_=x_grouped[h][:])

        def products(h, tiles):
            for n in tiles:
                acc = sums.tile([P, BANK], F32, name="acc")
                nc.tensor.matmul_mx(
                    out=acc[:],
                    lhsT=w2_codes[:, n * P : (n + 1) * P].bitcast(FP8X4),
                    lhsT_scale=w2_scales[:, n * P : (n + 1) * P],
                    rhs=x_codes[h][:].bitcast(FP8X4),
                    rhs_scale=x_scales[h][:],
                    start=True,
                    stop=True,
                )
                y = ring.tile([P, BANK], F32, name="y")
                nc.vector.tensor_tensor(y[:], acc[:], caps[n // 2][:, n % 2, half(h)], MULT)
                nc.sync.dma_start(out=out_0[n * P : (n + 1) * P, half(h)], in_=y[:])

        turn_page(last, 0)
        turn_x(last - 1, 0)
        turn_page(last, 1)
        turn_x(last, 0)
        turn_back(x_turned[0], x_grouped[0])
        quantize_x(0)
        products(0, range(N_TILES))
        turn_x(last - 1, 1)
        turn_x(last, 1)
        turn_back(x_turned[1], x_grouped[1])
        quantize_x(1)
        for c in range(CHUNKS):
            if c >= 2:
                turn_page(last, c)
            turn_back(page_turned[c], page_grouped[c])
        quantize_chunk(0)
        products(1, range(0, 2))
        quantize_chunk(1)
        products(1, range(2, 4))
        quantize_chunk(2)
        quantize_chunk(3)
        for q in range(4):
            nc.sync.dma_start(
                out=out_3[0, 4 * q : 4 * q + 4, :].bitcast(I32), in_=page_scales[32 * q : 32 * q + 4, :].bitcast(I32)
            )
        products(1, range(4, N_TILES))
